import numpy as np
import ml_dtypes


def mxq(x, axis, fmt="e4m3"):
    dtype, down = {"e4m3": (ml_dtypes.float8_e4m3fn, 7), "e5m2": (ml_dtypes.float8_e5m2, 14)}[fmt]
    v = np.moveaxis(np.asarray(x, np.float32).astype(ml_dtypes.bfloat16).astype(np.float64), axis, -1)
    blocks = v.reshape(v.shape[:-1] + (-1, 32))
    amax = np.abs(blocks).max(-1, keepdims=True)
    byte = np.maximum(np.where(amax > 0, np.frexp(amax)[1] - 1 + 127, 0) - down, 1)
    scale = np.exp2(byte - 127.0)
    codes = (blocks / scale).astype(np.float32).astype(dtype).astype(np.float64)
    return np.moveaxis((codes * scale).reshape(v.shape), -1, axis)


WIDE = False


def mx_kscale(k):
    if not WIDE:
        return np.ones(k)
    levels = np.array([30, -30])
    if k % 512:
        return np.exp2(np.random.permutation(np.resize(levels, k // 32))).repeat(32)
    a = np.empty((k // 512, 16))
    for p in range(k // 512):
        a[p, :8] = np.random.permutation(np.resize(levels, 8))
        for g in range(8):
            far = levels[np.abs(levels - a[p, g]) >= 10]
            a[p, g + 8] = far[np.random.randint(len(far))]
    return np.exp2(a.ravel()).repeat(32)


BF16 = ml_dtypes.bfloat16


def bf(x):
    return np.asarray(x, np.float32).astype(BF16)


def f64(x):
    return np.asarray(x).astype(np.float64)

E4M3FN = np.array([(-1.0 if i & 128 else 1.0) * ((1.0 + (i & 7) / 8.0) * 2.0 ** (((i >> 3) & 15) - 7) if i & 120 else (i & 7) * 2.0 ** -9) for i in range(256)])


def e4m3fn_bytes(y):
    return np.clip(np.asarray(y, np.float64), -448.0, 448.0).astype(np.float32).astype(ml_dtypes.float8_e4m3fn).view(np.uint8)


def e4m3fn_values(b):
    return E4M3FN[b]

def planes(Y):
    n, m = Y.shape
    b = f64(bf(Y)).reshape(n // 32, 32, m)
    amax = np.abs(b).max(1)
    byte = np.clip(np.where(amax > 0, np.frexp(amax)[1] - 1 + 127 - 7, 1), 1, 254)
    codes = (b * np.exp2(127.0 - byte)[:, None, :]).reshape(n, m).astype(np.float32).astype(ml_dtypes.float8_e4m3fn).view(np.uint8)
    words = codes.reshape(n // 512, 128, 4, m).transpose(0, 1, 3, 2)
    return np.ascontiguousarray(words), np.ascontiguousarray(byte.astype(np.uint8).reshape(n // 512, 16, m))


R, J, K, D, B = 1024, 2, 1536, 768, 32
T = R * J
FMAX = 448.0


def setup_inputs():
    s = mx_kscale(K)
    grad = np.random.randn(R, K) * np.exp(0.7 * np.random.randn(R, K))
    grad = grad * np.exp(0.8 * np.random.randn(R, 1)) * s[None, :]
    grad_scale = (np.abs(grad).reshape(R, K // B, B).max(axis=2) / FMAX).astype(np.float32)
    grad_bytes = e4m3fn_bytes(grad / np.repeat(f64(grad_scale), B, axis=1))
    w = bf(np.random.randn(K, J * D) * 1.5 / np.sqrt(K) / s[:, None])
    a = bf(np.random.randn(T, D))
    b = bf(np.random.randn(T, D))
    return {"grad_bytes": grad_bytes, "grad_scale": grad_scale, "w": w, "a": a, "b": b}

def reference(grad_bytes, grad_scale, w, a, b):
    grad = e4m3fn_values(grad_bytes) * np.repeat(f64(grad_scale), B, axis=1)
    a, b = f64(a), f64(b)
    gradq = mxq(grad, 1, "e5m2")
    wq = mxq(f64(w), 0, "e4m3")
    du = (gradq @ wq).reshape(T, D)
    h = 1.0 / (1.0 + np.exp(-b))
    da = du * h
    db = da * a * (1.0 - h)
    y = np.concatenate([da, db], axis=1)
    Y = y
    words, scales = planes(Y)
    return y, words, scales

@@ -1,0 +1,298 @@
+from contextlib import ExitStack
+
+import concourse.mybir as mybir
+from concourse.masks import make_identity
+
+R, K, D, TAPS = 1024, 1536, 768, 2
+FLOPS = 2 * R * K * TAPS * D
+
+F32 = mybir.dt.float32
+BF16 = mybir.dt.bfloat16
+I32 = mybir.dt.int32
+U32 = mybir.dt.uint32
+U8 = mybir.dt.uint8
+FP8 = mybir.dt.float8_e4m3fn
+E4M3X4 = mybir.dt.float8_e4m3fn_x4
+E5M2X4 = mybir.dt.float8_e5m2_x4
+ACT = mybir.ActivationFunctionType
+ALU = mybir.AluOpType
+
+P = 128
+PACK = 4
+KP = P * PACK
+PASSES = K // KP
+BLOCK = 32
+GROUPS = R * TAPS // KP
+ROWS = PACK // TAPS
+W = 256
+CHUNKS = D // W
+STEPS = GROUPS * CHUNKS
+UNITS = GROUPS * PASSES
+RUN = 4
+HEAD_UNITS = 6
+W_PIECES = (
+    (0, 0, 0, 1), (0, 0, 1, CHUNKS), (0, 1, 0, CHUNKS),
+    (1, 0, 0, CHUNKS), (1, 1, 0, CHUNKS), (2, 0, 0, CHUNKS), (2, 1, 0, CHUNKS),
+)
+
+
+def tile_strided_conv_glu_backward_b13_kernel(tc, grad_bytes, grad_scale, w, a, b, out_0, out_1, out_2):
+    nc = tc.nc
+    with ExitStack() as ctx:
+        keep = ctx.enter_context(tc.tile_pool(name="keep", bufs=1))
+        work = ctx.enter_context(tc.tile_pool(name="work", bufs=2))
+        psum = ctx.enter_context(tc.psum_pool(name="psum", bufs=4))
+        ctx.enter_context(tc.manual_schedule())
+
+        ident = keep.tile([P, P], F32, name="ident")
+        make_identity(nc, ident[:])
+
+        warm = keep.tile([P, 2], F32, name="warm")
+        nc.vector.memset(warm[:, 0:1], 0.0)
+        nc.scalar.activation(out=warm[:, 1:2], in_=warm[:, 0:1], func=ACT.Sigmoid)
+
+        w_codes = keep.tile([P, PASSES * TAPS * D], U32, name="w_codes", align_bytes=64)
+        w_scales = keep.tile([P, PASSES * TAPS * D], U8, name="w_scales", align_bytes=64)
+        g_codes = keep.tile([P, UNITS * ROWS * P], U32, name="g_codes", align_bytes=64)
+        g_scales = keep.tile([P, UNITS * ROWS * P], U8, name="g_scales", align_bytes=64)
+
+        gbytes, gscale, w_raw, a_sb, b_sb = {}, {}, {}, {}, {}
+        w_in, g_rows, g_bank, g_in = {}, {}, {}, {}
+        acc, h, q, half, half_in, y_codes, y_scales = {}, {}, {}, {}, {}, {}, {}
+
+        def load_grad(g, s0, s1):
+            piece = work.tile([P, ROWS, (s1 - s0) * KP], U8, name="gbytes", bufs=GROUPS + 1)
+            rows = grad_bytes[g * ROWS * P:(g + 1) * ROWS * P, s0 * KP:s1 * KP]
+            nc.sync.dma_start(out=piece[:], in_=rows.rearrange("(p e) k -> p e k", e=ROWS))
+            for s in range(s0, s1):
+                gbytes[g * PASSES + s] = piece[:, :, (s - s0) * KP:(s - s0 + 1) * KP]
+
+        def load_gscale(g0, g1):
+            piece = keep.tile([P, g1 - g0, ROWS * K // BLOCK], F32, name="gscale%d" % g0)
+            rows = grad_scale[g0 * ROWS * P:g1 * ROWS * P, :]
+            nc.sync.dma_start(out=piece[:], in_=rows.rearrange("(g p e) c -> p g (e c)", p=P, e=ROWS))
+            for g in range(g0, g1):
+                gscale[g] = piece[:, g - g0, :]
+
+        def load_w(u):
+            s, j, c0, c1 = W_PIECES[u]
+            w_raw[u] = work.tile([P, PACK, (c1 - c0) * W], BF16, name="w_raw", tag="wide", bufs=len(W_PIECES))
+            rows = w[s * KP:(s + 1) * KP, j * D + c0 * W:j * D + c1 * W]
+            nc.sync.dma_start(out=w_raw[u][:], in_=rows.rearrange("(p t) n -> p t n", t=PACK))
+
+        def load_tokens(src, tiles, name, g):
+            tiles[g] = work.tile([P, PACK, D], BF16, name=name, bufs=GROUPS)
+            nc.sync.dma_start(out=tiles[g][:], in_=src[g * KP:(g + 1) * KP, :].rearrange("(p t) d -> p t d", t=PACK))
+
+        def interleave_w(u):
+            s, j, c0, c1 = W_PIECES[u]
+            w_in[u] = work.tile([P, PACK * (c1 - c0) * W], BF16, name="w_in", align_bytes=64)
+            nc.vector.tensor_copy(
+                out=w_in[u][:].rearrange("p (c i t) -> p c t i", i=RUN, t=PACK),
+                in_=w_raw[u][:].rearrange("p t (c i) -> p c t i", i=RUN),
+            )
+
+        def quantize_w(u):
+            s, j, c0, c1 = W_PIECES[u]
+            for c in range(c0, c1):
+                at = ((s * CHUNKS + c) * TAPS + j) * W
+                nc.vector.quantize_mx(
+                    out=w_codes[:, at:at + W].bitcast(E4M3X4),
+                    scales=w_scales[:, at:at + W],
+                    in_=w_in[u][:, (c - c0) * W * PACK:(c - c0 + 1) * W * PACK],
+                )
+
+        def scale_grad(u):
+            g, s = divmod(u, PASSES)
+            g_rows[u] = work.tile([P, ROWS * KP], BF16, name="g_rows", bufs=3)
+            for e in range(ROWS):
+                for i in range(KP // BLOCK):
+                    col = (e * K + s * KP) // BLOCK + i
+                    nc.scalar.activation(
+                        out=g_rows[u][:, e * KP + i * BLOCK:e * KP + (i + 1) * BLOCK],
+                        in_=gbytes[u][:, e, i * BLOCK:(i + 1) * BLOCK].bitcast(FP8),
+                        func=ACT.Copy,
+                        scale=gscale[g][:, col:col + 1],
+                    )
+
+        def turn_grad(u):
+            g_bank[u] = psum.tile([P, ROWS * 2, P], F32, name="g_bank", bufs=3)
+            words = g_rows[u][:].bitcast(F32)
+            for e in range(ROWS):
+                for v in range(2):
+                    nc.tensor.transpose(g_bank[u][:, 2 * e + v, :], words[:, e * 2 * P + v:(e + 1) * 2 * P:2], ident[:])
+
+        def copy_grad(u):
+            g_in[u] = work.tile([P, ROWS * KP], BF16, name="g_in", bufs=4, align_bytes=64)
+            nc.scalar.copy(
+                out=g_in[u][:].bitcast(F32).rearrange("p (e r v) -> p e r v", e=ROWS, v=2),
+                in_=g_bank[u][:].rearrange("p (e v) r -> p e r v", v=2),
+            )
+
+        def quantize_grad(u):
+            cols = slice(u * ROWS * P, (u + 1) * ROWS * P)
+            nc.vector.quantize_mx(out=g_codes[:, cols].bitcast(E5M2X4), scales=g_scales[:, cols], in_=g_in[u][:])
+
+        def multiply(n):
+            g, c = divmod(n, CHUNKS)
+            for e in range(ROWS):
+                acc[n, e] = psum.tile([P, TAPS * W], F32, name="acc", bufs=4)
+                for s in range(PASSES):
+                    m = ((g * PASSES + s) * ROWS + e) * P
+                    at = (s * CHUNKS + c) * TAPS * W
+                    nc.tensor.matmul_mx(
+                        out=acc[n, e][:],
+                        lhsT=g_codes[:, m:m + P].bitcast(E5M2X4),
+                        lhsT_scale=g_scales[:, m:m + P],
+                        rhs=w_codes[:, at:at + TAPS * W].bitcast(E4M3X4),
+                        rhs_scale=w_scales[:, at:at + TAPS * W],
+                        start=(s == 0),
+                        stop=(s == PASSES - 1),
+                    )
+
+        def sigmoid(n):
+            g, c = divmod(n, CHUNKS)
+            h[n] = work.tile([P, PACK, W], F32, name="h", bufs=4)
+            nc.scalar.activation(out=h[n][:], in_=b_sb[g][:, :, c * W:(c + 1) * W], func=ACT.Sigmoid)
+
+        def gate_factor(n):
+            g, c = divmod(n, CHUNKS)
+            q[n] = work.tile([P, PACK, W], F32, name="q")
+            nc.vector.scalar_tensor_tensor(
+                out=q[n][:], in0=h[n][:], scalar=1.0, in1=a_sb[g][:, :, c * W:(c + 1) * W],
+                op0=ALU.subtract, op1=ALU.mult,
+            )
+
+        def store_half(n, x):
+            g, c = divmod(n, CHUNKS)
+            rows = out_0[g * KP:(g + 1) * KP, x * D + c * W:x * D + (c + 1) * W]
+            nc.sync.dma_start(out=rows.rearrange("(p t) d -> p t d", t=PACK), in_=half[n, x][:])
+
+        def value_half(n):
+            half[n, 0] = work.tile([P, PACK, W], F32, name="da", tag="wide", bufs=len(W_PIECES))
+            for e in range(ROWS):
+                nc.vector.tensor_tensor(
+                    out=half[n, 0][:, e * TAPS:(e + 1) * TAPS, :].rearrange("p j d -> p (j d)"),
+                    in0=acc[n, e][:],
+                    in1=h[n][:, e * TAPS:(e + 1) * TAPS, :].rearrange("p j d -> p (j d)"),
+                    op=ALU.mult,
+                )
+            store_half(n, 0)
+
+        def gate_half(n):
+            half[n, 1] = work.tile([P, PACK, W], F32, name="db", bufs=4)
+            nc.vector.scalar_tensor_tensor(
+                out=half[n, 1][:], in0=half[n, 0][:], scalar=-1.0, in1=q[n][:], op0=ALU.mult, op1=ALU.mult,
+            )
+            store_half(n, 1)
+
+        def interleave_y(n, x, on_vector):
+            half_in[n, x] = work.tile([P, PACK * W], BF16, name="half_in", bufs=5, align_bytes=64)
+            dst = half_in[n, x][:].rearrange("p (c i t) -> p c t i", i=RUN, t=PACK)
+            src = half[n, x][:].rearrange("p t (c i) -> p c t i", i=RUN)
+            if on_vector:
+                nc.vector.tensor_copy(out=dst, in_=src)
+            else:
+                nc.scalar.copy(out=dst, in_=src)
+
+        def quantize_y(n, x):
+            g, c = divmod(n, CHUNKS)
+            if c == 0 and x == 0:
+                y_codes[g] = work.tile([P, TAPS * D], U32, name="y_codes", align_bytes=64)
+                y_scales[g] = work.tile([P, TAPS * D], U8, name="y_scales", align_bytes=64)
+            cols = slice(x * D + c * W, x * D + (c + 1) * W)
+            nc.vector.quantize_mx(
+                out=y_codes[g][:, cols].bitcast(E4M3X4), scales=y_scales[g][:, cols], in_=half_in[n, x][:],
+            )
+
+        def store_planes(n):
+            g, c = divmod(n, CHUNKS)
+            words = out_1[g].rearrange("p m t -> p (m t)").bitcast(I32)
+            codes = y_codes[g][:].bitcast(I32)
+            if g == GROUPS - 1:
+                nc.sync.dma_start(
+                    out=words.rearrange("p (x d) -> p x d", x=2)[:, :, c * W:(c + 1) * W],
+                    in_=codes.rearrange("p (x d) -> p x d", x=2)[:, :, c * W:(c + 1) * W],
+                )
+            elif c == CHUNKS - 1:
+                nc.sync.dma_start(out=words, in_=codes)
+            if c == CHUNKS - 1:
+                for quad in range(4):
+                    nc.sync.dma_start(
+                        out=out_2[g, 4 * quad:4 * quad + 4, :].bitcast(I32),
+                        in_=y_scales[g][32 * quad:32 * quad + 4, :].bitcast(I32),
+                    )
+
+        load_gscale(0, 1)
+        load_grad(0, 0, 1)
+        load_w(0)
+        load_w(1)
+        load_grad(0, 1, PASSES)
+        load_w(2)
+        load_tokens(b, b_sb, "b_sb", 0)
+        load_w(3)
+        load_gscale(1, GROUPS)
+        load_grad(1, 0, PASSES)
+        load_w(4)
+        load_w(5)
+        load_w(6)
+        load_tokens(a, a_sb, "a_sb", 0)
+        load_grad(2, 0, PASSES)
+        load_tokens(b, b_sb, "b_sb", 1)
+        load_grad(3, 0, PASSES)
+        load_tokens(a, a_sb, "a_sb", 1)
+        for g in range(2, GROUPS):
+            load_tokens(b, b_sb, "b_sb", g)
+            load_tokens(a, a_sb, "a_sb", g)
+
+        interleave_w(0)
+        for u in range(HEAD_UNITS):
+            scale_grad(u)
+            turn_grad(u)
+            if u > 0:
+                copy_grad(u - 1)
+            if u in (2, 3):
+                sigmoid(u - 2)
+            if u == 0:
+                quantize_w(0)
+            interleave_w(u + 1)
+            if u > 0:
+                quantize_w(u)
+            if u > 1:
+                quantize_grad(u - 2)
+        gate_factor(0)
+        quantize_w(HEAD_UNITS)
+        multiply(0)
+
+        for n in range(STEPS):
+            unit = HEAD_UNITS + n
+            last = n == STEPS - 1
+            if not last:
+                multiply(n + 1)
+            if n > 0:
+                interleave_y(n - 1, 1, False)
+            if unit - 1 < UNITS:
+                copy_grad(unit - 1)
+            if n + 2 < STEPS:
+                sigmoid(n + 2)
+            if unit < UNITS:
+                scale_grad(unit)
+                turn_grad(unit)
+            value_half(n)
+            if not last:
+                gate_factor(n + 1)
+            else:
+                quantize_y(n - 1, 0)
+            gate_half(n)
+            interleave_y(n, 0, unit < UNITS)
+            if n > 0:
+                if not last:
+                    quantize_y(n - 1, 0)
+                quantize_y(n - 1, 1)
+                store_planes(n - 1)
+            if unit - 2 < UNITS:
+                quantize_grad(unit - 2)
+        interleave_y(STEPS - 1, 1, True)
+        quantize_y(STEPS - 1, 0)
+        quantize_y(STEPS - 1, 1)
+        store_planes(STEPS - 1)

@@ -29,7 +29,12 @@ CHUNKS = D // W
 STEPS = GROUPS * CHUNKS
 UNITS = GROUPS * PASSES
 RUN = 4
-HEAD_UNITS = 6
+HEAD_UNITS = 8
+VECTOR_STEPS = (2, 4, 6)
+UNIT_STRIDE = 2
+WHOLE_GROUPS = 2
+SIG_TICKS = (4, 6)
+LOADS = "w2 w3 s1 g1 w4 b0 w5 w6 g2 a0 b1 g3 a1 b2 a2 a3"
 W_PIECES = (
     (0, 0, 0, 1), (0, 0, 1, CHUNKS), (0, 1, 0, CHUNKS),
     (1, 0, 0, CHUNKS), (1, 1, 0, CHUNKS), (2, 0, 0, CHUNKS), (2, 1, 0, CHUNKS),
@@ -80,8 +85,8 @@ def tile_strided_conv_glu_backward_b13_kernel(tc, grad_bytes, grad_scale, w, a, 
             rows = w[s * KP:(s + 1) * KP, j * D + c0 * W:j * D + c1 * W]
             nc.sync.dma_start(out=w_raw[u][:], in_=rows.rearrange("(p t) n -> p t n", t=PACK))
 
-        def load_tokens(src, tiles, name, g):
-            tiles[g] = work.tile([P, PACK, D], BF16, name=name, bufs=GROUPS)
+        def load_tokens(src, tiles, name, g, bufs):
+            tiles[g] = work.tile([P, PACK, D], BF16, name=name, bufs=bufs)
             nc.sync.dma_start(out=tiles[g][:], in_=src[g * KP:(g + 1) * KP, :].rearrange("(p t) d -> p t d", t=PACK))
 
         def interleave_w(u):
@@ -92,9 +97,9 @@ def tile_strided_conv_glu_backward_b13_kernel(tc, grad_bytes, grad_scale, w, a, 
                 in_=w_raw[u][:].rearrange("p t (c i) -> p c t i", i=RUN),
             )
 
-        def quantize_w(u):
+        def quantize_w(u, first=0, stop=CHUNKS):
             s, j, c0, c1 = W_PIECES[u]
-            for c in range(c0, c1):
+            for c in range(max(c0, first), min(c1, stop)):
                 at = ((s * CHUNKS + c) * TAPS + j) * W
                 nc.vector.quantize_mx(
                     out=w_codes[:, at:at + W].bitcast(E4M3X4),
@@ -152,7 +157,7 @@ def tile_strided_conv_glu_backward_b13_kernel(tc, grad_bytes, grad_scale, w, a, 
 
         def sigmoid(n):
             g, c = divmod(n, CHUNKS)
-            h[n] = work.tile([P, PACK, W], F32, name="h", bufs=4)
+            h[n] = work.tile([P, PACK, W], F32, name="h", bufs=len(SIG_TICKS) + 1)
             nc.scalar.activation(out=h[n][:], in_=b_sb[g][:, :, c * W:(c + 1) * W], func=ACT.Sigmoid)
 
         def gate_factor(n):
@@ -209,7 +214,7 @@ def tile_strided_conv_glu_backward_b13_kernel(tc, grad_bytes, grad_scale, w, a, 
             g, c = divmod(n, CHUNKS)
             words = out_1[g].rearrange("p m t -> p (m t)").bitcast(I32)
             codes = y_codes[g][:].bitcast(I32)
-            if g == GROUPS - 1:
+            if g >= WHOLE_GROUPS:
                 nc.sync.dma_start(
                     out=words.rearrange("p (x d) -> p x d", x=2)[:, :, c * W:(c + 1) * W],
                     in_=codes.rearrange("p (x d) -> p x d", x=2)[:, :, c * W:(c + 1) * W],
@@ -217,8 +222,9 @@ def tile_strided_conv_glu_backward_b13_kernel(tc, grad_bytes, grad_scale, w, a, 
             elif c == CHUNKS - 1:
                 nc.sync.dma_start(out=words, in_=codes)
             if c == CHUNKS - 1:
+                queue = nc.scalar if n == STEPS - 1 else nc.sync
                 for quad in range(4):
-                    nc.sync.dma_start(
+                    queue.dma_start(
                         out=out_2[g, 4 * quad:4 * quad + 4, :].bitcast(I32),
                         in_=y_scales[g][32 * quad:32 * quad + 4, :].bitcast(I32),
                     )
@@ -228,70 +234,81 @@ def tile_strided_conv_glu_backward_b13_kernel(tc, grad_bytes, grad_scale, w, a, 
         load_w(0)
         load_w(1)
         load_grad(0, 1, PASSES)
-        load_w(2)
-        load_tokens(b, b_sb, "b_sb", 0)
-        load_w(3)
-        load_gscale(1, GROUPS)
-        load_grad(1, 0, PASSES)
-        load_w(4)
-        load_w(5)
-        load_w(6)
-        load_tokens(a, a_sb, "a_sb", 0)
-        load_grad(2, 0, PASSES)
-        load_tokens(b, b_sb, "b_sb", 1)
-        load_grad(3, 0, PASSES)
-        load_tokens(a, a_sb, "a_sb", 1)
-        for g in range(2, GROUPS):
-            load_tokens(b, b_sb, "b_sb", g)
-            load_tokens(a, a_sb, "a_sb", g)
+        for item in LOADS.split():
+            i = int(item[1])
+            if item[0] == "w":
+                load_w(i)
+            elif item[0] == "s":
+                load_gscale(1, GROUPS)
+            elif item[0] == "g":
+                load_grad(i, 0, PASSES)
+            elif item[0] == "a":
+                load_tokens(a, a_sb, "a_sb", i, 4)
+            else:
+                load_tokens(b, b_sb, "b_sb", i, 3)
 
+        last_piece = len(W_PIECES) - 1
+        ahead = len(SIG_TICKS)
         interleave_w(0)
         for u in range(HEAD_UNITS):
             scale_grad(u)
-            turn_grad(u)
             if u > 0:
                 copy_grad(u - 1)
-            if u in (2, 3):
-                sigmoid(u - 2)
+            if u in SIG_TICKS:
+                sigmoid(SIG_TICKS.index(u))
             if u == 0:
                 quantize_w(0)
-            interleave_w(u + 1)
-            if u > 0:
-                quantize_w(u)
+            if u < last_piece:
+                interleave_w(u + 1)
+                if u > 0:
+                    quantize_w(u)
+            if u == last_piece:
+                quantize_w(last_piece, 0, 1)
+                gate_factor(0)
+                quantize_w(last_piece, 1, CHUNKS)
             if u > 1:
                 quantize_grad(u - 2)
-        gate_factor(0)
-        quantize_w(HEAD_UNITS)
-        multiply(0)
+            if u == HEAD_UNITS - 1:
+                multiply(0)
+            turn_grad(u)
 
         for n in range(STEPS):
-            unit = HEAD_UNITS + n
             last = n == STEPS - 1
             if not last:
                 multiply(n + 1)
             if n > 0:
                 interleave_y(n - 1, 1, False)
-            if unit - 1 < UNITS:
-                copy_grad(unit - 1)
-            if n + 2 < STEPS:
-                sigmoid(n + 2)
-            if unit < UNITS:
-                scale_grad(unit)
-                turn_grad(unit)
+            if n == 0 or (n - 1) % UNIT_STRIDE == 0:
+                fresh = HEAD_UNITS - 1 if n == 0 else HEAD_UNITS + (n - 1) // UNIT_STRIDE
+                if fresh < UNITS:
+                    copy_grad(fresh)
+            if n % UNIT_STRIDE == 0 and HEAD_UNITS + n // UNIT_STRIDE < UNITS:
+                scale_grad(HEAD_UNITS + n // UNIT_STRIDE)
+                turn_grad(HEAD_UNITS + n // UNIT_STRIDE)
+            if n + ahead < STEPS:
+                sigmoid(n + ahead)
+            if n == 0:
+                load_tokens(b, b_sb, "b_sb", 3, 3)
             value_half(n)
             if not last:
                 gate_factor(n + 1)
             else:
                 quantize_y(n - 1, 0)
+            if n not in VECTOR_STEPS:
+                interleave_y(n, 0, False)
             gate_half(n)
-            interleave_y(n, 0, unit < UNITS)
+            if n in VECTOR_STEPS:
+                interleave_y(n, 0, True)
             if n > 0:
                 if not last:
                     quantize_y(n - 1, 0)
                 quantize_y(n - 1, 1)
                 store_planes(n - 1)
-            if unit - 2 < UNITS:
-                quantize_grad(unit - 2)
+            if n == 0:
+                quantize_grad(HEAD_UNITS - 2)
+                quantize_grad(HEAD_UNITS - 1)
+            elif (n - 1) % UNIT_STRIDE == 0 and HEAD_UNITS + (n - 1) // UNIT_STRIDE < UNITS:
+                quantize_grad(HEAD_UNITS + (n - 1) // UNIT_STRIDE)
         interleave_y(STEPS - 1, 1, True)
         quantize_y(STEPS - 1, 0)
         quantize_y(STEPS - 1, 1)

@@ -23,22 +23,29 @@ KP = P * PACK
 PASSES = K // KP
 BLOCK = 32
 GROUPS = R * TAPS // KP
+LAST = GROUPS - 1
 ROWS = PACK // TAPS
+PAIRS = PACK // 2
 W = 256
 CHUNKS = D // W
-STEPS = GROUPS * CHUNKS
 UNITS = GROUPS * PASSES
+QUADS = 4
 RUN = 4
+
 HEAD_UNITS = 8
-VECTOR_STEPS = (2, 4, 6)
-UNIT_STRIDE = 2
-WHOLE_GROUPS = 2
-SIG_TICKS = (4, 6)
-LOADS = "w2 w3 s1 g1 w4 b0 w5 w6 g2 a0 b1 g3 a1 b2 a2 a3"
-W_PIECES = (
-    (0, 0, 0, 1), (0, 0, 1, CHUNKS), (0, 1, 0, CHUNKS),
-    (1, 0, 0, CHUNKS), (1, 1, 0, CHUNKS), (2, 0, 0, CHUNKS), (2, 1, 0, CHUNKS),
-)
+SIGMOID_TICKS = (4, 6, 7)
+EARLY_PASS_TICKS = (4, 5)
+UNITS_PER_ROUND = 2
+GPSIMD_COLS = D // 2
+
+WIDE_BUFS = 4
+ACC_BUFS = ROWS * CHUNKS
+BYTES_BUFS = 3
+B_BUFS = 3
+H_BUFS = CHUNKS + 1
+G_ROWS_BUFS = 3
+G_IN_BUFS = 4
+Y_IN_BUFS = 3
 
 
 def tile_strided_conv_glu_backward_b13_kernel(tc, grad_bytes, grad_scale, w, a, b, out_0, out_1, out_2):
@@ -46,27 +53,23 @@ def tile_strided_conv_glu_backward_b13_kernel(tc, grad_bytes, grad_scale, w, a, 
     with ExitStack() as ctx:
         keep = ctx.enter_context(tc.tile_pool(name="keep", bufs=1))
         work = ctx.enter_context(tc.tile_pool(name="work", bufs=2))
-        psum = ctx.enter_context(tc.psum_pool(name="psum", bufs=4))
+        psum = ctx.enter_context(tc.psum_pool(name="psum", bufs=2))
         ctx.enter_context(tc.manual_schedule())
 
         ident = keep.tile([P, P], F32, name="ident")
         make_identity(nc, ident[:])
-
-        warm = keep.tile([P, 2], F32, name="warm")
-        nc.vector.memset(warm[:, 0:1], 0.0)
-        nc.scalar.activation(out=warm[:, 1:2], in_=warm[:, 0:1], func=ACT.Sigmoid)
 
         w_codes = keep.tile([P, PASSES * TAPS * D], U32, name="w_codes", align_bytes=64)
         w_scales = keep.tile([P, PASSES * TAPS * D], U8, name="w_scales", align_bytes=64)
         g_codes = keep.tile([P, UNITS * ROWS * P], U32, name="g_codes", align_bytes=64)
         g_scales = keep.tile([P, UNITS * ROWS * P], U8, name="g_scales", align_bytes=64)
 
-        gbytes, gscale, w_raw, a_sb, b_sb = {}, {}, {}, {}, {}
-        w_in, g_rows, g_bank, g_in = {}, {}, {}, {}
-        acc, h, q, half, half_in, y_codes, y_scales = {}, {}, {}, {}, {}, {}, {}
+        gbytes, gscale, a_sb, b_sb = {}, {}, {}, {}
+        w_raw, w_in, g_rows, g_bank, g_in = [], {}, {}, {}, {}
+        acc, h, q, y, y_in, y_codes, y_scales = {}, {}, {}, {}, {}, {}, {}
 
         def load_grad(g, s0, s1):
-            piece = work.tile([P, ROWS, (s1 - s0) * KP], U8, name="gbytes", bufs=GROUPS + 1)
+            piece = work.tile([P, ROWS, (s1 - s0) * KP], U8, name="gbytes" if g else "gbytes_head", bufs=BYTES_BUFS)
             rows = grad_bytes[g * ROWS * P:(g + 1) * ROWS * P, s0 * KP:s1 * KP]
             nc.sync.dma_start(out=piece[:], in_=rows.rearrange("(p e) k -> p e k", e=ROWS))
             for s in range(s0, s1):
@@ -79,237 +82,303 @@ def tile_strided_conv_glu_backward_b13_kernel(tc, grad_bytes, grad_scale, w, a, 
             for g in range(g0, g1):
                 gscale[g] = piece[:, g - g0, :]
 
-        def load_w(u):
-            s, j, c0, c1 = W_PIECES[u]
-            w_raw[u] = work.tile([P, PACK, (c1 - c0) * W], BF16, name="w_raw", tag="wide", bufs=len(W_PIECES))
-            rows = w[s * KP:(s + 1) * KP, j * D + c0 * W:j * D + c1 * W]
-            nc.sync.dma_start(out=w_raw[u][:], in_=rows.rearrange("(p t) n -> p t n", t=PACK))
+        def load_w(s, lo, hi):
+            if s == 0:
+                piece = keep.tile([P, PACK, hi - lo], BF16, name="w_first%d" % lo)
+            else:
+                piece = work.tile([P, PACK, hi - lo], BF16, name="w_pass", tag="wide", bufs=WIDE_BUFS)
+            rows = w[s * KP:(s + 1) * KP, lo:hi]
+            nc.sync.dma_start(out=piece[:], in_=rows.rearrange("(p t) n -> p t n", t=PACK))
+            w_raw.append((s, lo, hi, piece))
 
-        def load_tokens(src, tiles, name, g, bufs):
-            tiles[g] = work.tile([P, PACK, D], BF16, name=name, bufs=bufs)
-            nc.sync.dma_start(out=tiles[g][:], in_=src[g * KP:(g + 1) * KP, :].rearrange("(p t) d -> p t d", t=PACK))
+        def load_tokens(src, tiles, name, bufs, g, lo=0, hi=PACK * D):
+            if lo == 0:
+                tiles[g] = work.tile([P, PACK, D], BF16, name=name, bufs=bufs)
+            rows = src[g * KP:(g + 1) * KP, :].rearrange("(p t) d -> p (t d)", t=PACK)
+            nc.sync.dma_start(out=tiles[g][:].rearrange("p t d -> p (t d)")[:, lo:hi], in_=rows[:, lo:hi])
 
-        def interleave_w(u):
-            s, j, c0, c1 = W_PIECES[u]
-            w_in[u] = work.tile([P, PACK * (c1 - c0) * W], BF16, name="w_in", align_bytes=64)
+        def load_a(g):
+            load_tokens(a, a_sb, "a_sb", GROUPS, g)
+
+        def load_b(g, lo=0, hi=PACK * D):
+            load_tokens(b, b_sb, "b_sb", B_BUFS, g, lo, hi)
+
+        def interleave_w(i):
+            s, lo, hi, piece = w_raw[i]
+            w_in[i] = work.tile([P, PACK * (hi - lo)], BF16, name="w_in", align_bytes=64)
             nc.vector.tensor_copy(
-                out=w_in[u][:].rearrange("p (c i t) -> p c t i", i=RUN, t=PACK),
-                in_=w_raw[u][:].rearrange("p t (c i) -> p c t i", i=RUN),
+                out=w_in[i][:].rearrange("p (m i t) -> p m t i", i=RUN, t=PACK),
+                in_=piece[:].rearrange("p t (m i) -> p m t i", i=RUN),
             )
 
-        def quantize_w(u, first=0, stop=CHUNKS):
-            s, j, c0, c1 = W_PIECES[u]
-            for c in range(max(c0, first), min(c1, stop)):
+        def quantize_w(i, first=0, stop=CHUNKS):
+            s, lo, hi, piece = w_raw[i]
+            for m in range(first, min(stop, (hi - lo) // W)):
+                j, c = divmod(lo // W + m, CHUNKS)
                 at = ((s * CHUNKS + c) * TAPS + j) * W
                 nc.vector.quantize_mx(
                     out=w_codes[:, at:at + W].bitcast(E4M3X4),
                     scales=w_scales[:, at:at + W],
-                    in_=w_in[u][:, (c - c0) * W * PACK:(c - c0 + 1) * W * PACK],
+                    in_=w_in[i][:, m * W * PACK:(m + 1) * W * PACK],
                 )
 
         def scale_grad(u):
             g, s = divmod(u, PASSES)
-            g_rows[u] = work.tile([P, ROWS * KP], BF16, name="g_rows", bufs=3)
+            g_rows[u] = work.tile([P, ROWS * KP], BF16, name="g_rows", bufs=G_ROWS_BUFS)
             for e in range(ROWS):
-                for i in range(KP // BLOCK):
-                    col = (e * K + s * KP) // BLOCK + i
+                for m in range(KP // BLOCK):
+                    col = (e * K + s * KP) // BLOCK + m
                     nc.scalar.activation(
-                        out=g_rows[u][:, e * KP + i * BLOCK:e * KP + (i + 1) * BLOCK],
-                        in_=gbytes[u][:, e, i * BLOCK:(i + 1) * BLOCK].bitcast(FP8),
+                        out=g_rows[u][:, e * KP + m * BLOCK:e * KP + (m + 1) * BLOCK],
+                        in_=gbytes[u][:, e, m * BLOCK:(m + 1) * BLOCK].bitcast(FP8),
                         func=ACT.Copy,
                         scale=gscale[g][:, col:col + 1],
                     )
 
         def turn_grad(u):
-            g_bank[u] = psum.tile([P, ROWS * 2, P], F32, name="g_bank", bufs=3)
+            g_bank[u] = psum.tile([P, ROWS * PAIRS, P], F32, name="g_bank")
             words = g_rows[u][:].bitcast(F32)
             for e in range(ROWS):
-                for v in range(2):
-                    nc.tensor.transpose(g_bank[u][:, 2 * e + v, :], words[:, e * 2 * P + v:(e + 1) * 2 * P:2], ident[:])
+                for v in range(PAIRS):
+                    nc.tensor.transpose(
+                        g_bank[u][:, PAIRS * e + v, :], words[:, e * PAIRS * P + v:(e + 1) * PAIRS * P:PAIRS], ident[:]
+                    )
 
         def copy_grad(u):
-            g_in[u] = work.tile([P, ROWS * KP], BF16, name="g_in", bufs=4, align_bytes=64)
+            g_in[u] = work.tile([P, ROWS * KP], BF16, name="g_in", bufs=G_IN_BUFS, align_bytes=64)
             nc.scalar.copy(
-                out=g_in[u][:].bitcast(F32).rearrange("p (e r v) -> p e r v", e=ROWS, v=2),
-                in_=g_bank[u][:].rearrange("p (e v) r -> p e r v", v=2),
+                out=g_in[u][:].bitcast(F32).rearrange("p (e r v) -> p e r v", e=ROWS, v=PAIRS),
+                in_=g_bank[u][:].rearrange("p (e v) r -> p e r v", v=PAIRS),
             )
 
         def quantize_grad(u):
             cols = slice(u * ROWS * P, (u + 1) * ROWS * P)
             nc.vector.quantize_mx(out=g_codes[:, cols].bitcast(E5M2X4), scales=g_scales[:, cols], in_=g_in[u][:])
 
-        def multiply(n):
-            g, c = divmod(n, CHUNKS)
-            for e in range(ROWS):
-                acc[n, e] = psum.tile([P, TAPS * W], F32, name="acc", bufs=4)
-                for s in range(PASSES):
-                    m = ((g * PASSES + s) * ROWS + e) * P
+        def banks(g):
+            if g == LAST:
+                return [(e, c) for e in range(ROWS) for c in range(CHUNKS)]
+            return [(e, c) for c in range(CHUNKS) for e in range(ROWS)]
+
+        def multiply(g, s0=0, s1=PASSES):
+            for e, c in banks(g):
+                if s0 == 0:
+                    acc[g, e, c] = psum.tile([P, TAPS * W], F32, name="acc", bufs=ACC_BUFS)
+                for s in range(s0, s1):
+                    rows = ((g * PASSES + s) * ROWS + e) * P
                     at = (s * CHUNKS + c) * TAPS * W
                     nc.tensor.matmul_mx(
-                        out=acc[n, e][:],
-                        lhsT=g_codes[:, m:m + P].bitcast(E5M2X4),
-                        lhsT_scale=g_scales[:, m:m + P],
+                        out=acc[g, e, c][:],
+                        lhsT=g_codes[:, rows:rows + P].bitcast(E5M2X4),
+                        lhsT_scale=g_scales[:, rows:rows + P],
                         rhs=w_codes[:, at:at + TAPS * W].bitcast(E4M3X4),
                         rhs_scale=w_scales[:, at:at + TAPS * W],
                         start=(s == 0),
                         stop=(s == PASSES - 1),
                     )
 
-        def sigmoid(n):
-            g, c = divmod(n, CHUNKS)
-            h[n] = work.tile([P, PACK, W], F32, name="h", bufs=len(SIG_TICKS) + 1)
-            nc.scalar.activation(out=h[n][:], in_=b_sb[g][:, :, c * W:(c + 1) * W], func=ACT.Sigmoid)
+        def sigmoid(g, c, t0=0, t1=PACK):
+            if t0 == 0:
+                h[g, c] = work.tile([P, PACK, W], F32, name="h", bufs=H_BUFS)
+            nc.scalar.activation(out=h[g, c][:, t0:t1, :], in_=b_sb[g][:, t0:t1, c * W:(c + 1) * W], func=ACT.Sigmoid)
 
-        def gate_factor(n):
-            g, c = divmod(n, CHUNKS)
-            q[n] = work.tile([P, PACK, W], F32, name="q")
+        def gate_factor(g, c):
+            q[g, c] = work.tile([P, PACK, W], F32, name="q")
             nc.vector.scalar_tensor_tensor(
-                out=q[n][:], in0=h[n][:], scalar=1.0, in1=a_sb[g][:, :, c * W:(c + 1) * W],
+                out=q[g, c][:], in0=h[g, c][:], scalar=1.0, in1=a_sb[g][:, :, c * W:(c + 1) * W],
                 op0=ALU.subtract, op1=ALU.mult,
             )
 
-        def store_half(n, x):
-            g, c = divmod(n, CHUNKS)
-            rows = out_0[g * KP:(g + 1) * KP, x * D + c * W:x * D + (c + 1) * W]
-            nc.sync.dma_start(out=rows.rearrange("(p t) d -> p t d", t=PACK), in_=half[n, x][:])
+        def store_y(g, x, lo, hi, t0=0, t1=PACK):
+            rows = out_0[g * KP:(g + 1) * KP, x * D + lo:x * D + hi].rearrange("(p t) d -> p t d", t=PACK)
+            nc.sync.dma_start(out=rows[:, t0:t1, :], in_=y[g, x][:, t0:t1, lo:hi])
 
-        def value_half(n):
-            half[n, 0] = work.tile([P, PACK, W], F32, name="da", tag="wide", bufs=len(W_PIECES))
-            for e in range(ROWS):
+        def value_half(g):
+            y[g, 0] = work.tile([P, PACK, D], F32, name="da", tag="wide", bufs=WIDE_BUFS)
+            for e, c in banks(g):
                 nc.vector.tensor_tensor(
-                    out=half[n, 0][:, e * TAPS:(e + 1) * TAPS, :].rearrange("p j d -> p (j d)"),
-                    in0=acc[n, e][:],
-                    in1=h[n][:, e * TAPS:(e + 1) * TAPS, :].rearrange("p j d -> p (j d)"),
+                    out=y[g, 0][:, e * TAPS:(e + 1) * TAPS, c * W:(c + 1) * W],
+                    in0=acc[g, e, c][:].rearrange("p (j d) -> p j d", j=TAPS),
+                    in1=h[g, c][:, e * TAPS:(e + 1) * TAPS, :],
                     op=ALU.mult,
                 )
-            store_half(n, 0)
+                if c == CHUNKS - 1:
+                    store_y(g, 0, 0, D, e * TAPS, (e + 1) * TAPS)
 
-        def gate_half(n):
-            half[n, 1] = work.tile([P, PACK, W], F32, name="db", bufs=4)
+        def gate_half(g, lo, hi):
+            c = lo // W
+            if lo == 0:
+                y[g, 1] = work.tile([P, PACK, D], F32, name="db", tag="wide", bufs=WIDE_BUFS)
             nc.vector.scalar_tensor_tensor(
-                out=half[n, 1][:], in0=half[n, 0][:], scalar=-1.0, in1=q[n][:], op0=ALU.mult, op1=ALU.mult,
-            )
-            store_half(n, 1)
-
-        def interleave_y(n, x, on_vector):
-            half_in[n, x] = work.tile([P, PACK * W], BF16, name="half_in", bufs=5, align_bytes=64)
-            dst = half_in[n, x][:].rearrange("p (c i t) -> p c t i", i=RUN, t=PACK)
-            src = half[n, x][:].rearrange("p t (c i) -> p c t i", i=RUN)
-            if on_vector:
-                nc.vector.tensor_copy(out=dst, in_=src)
-            else:
-                nc.scalar.copy(out=dst, in_=src)
-
-        def quantize_y(n, x):
-            g, c = divmod(n, CHUNKS)
-            if c == 0 and x == 0:
-                y_codes[g] = work.tile([P, TAPS * D], U32, name="y_codes", align_bytes=64)
-                y_scales[g] = work.tile([P, TAPS * D], U8, name="y_scales", align_bytes=64)
-            cols = slice(x * D + c * W, x * D + (c + 1) * W)
-            nc.vector.quantize_mx(
-                out=y_codes[g][:, cols].bitcast(E4M3X4), scales=y_scales[g][:, cols], in_=half_in[n, x][:],
+                out=y[g, 1][:, :, lo:hi], in0=y[g, 0][:, :, lo:hi], scalar=-1.0,
+                in1=q[g, c][:, :, lo - c * W:hi - c * W], op0=ALU.mult, op1=ALU.mult,
             )
 
-        def store_planes(n):
-            g, c = divmod(n, CHUNKS)
-            words = out_1[g].rearrange("p m t -> p (m t)").bitcast(I32)
-            codes = y_codes[g][:].bitcast(I32)
-            if g >= WHOLE_GROUPS:
-                nc.sync.dma_start(
-                    out=words.rearrange("p (x d) -> p x d", x=2)[:, :, c * W:(c + 1) * W],
-                    in_=codes.rearrange("p (x d) -> p x d", x=2)[:, :, c * W:(c + 1) * W],
+        def interleave_y(g, x, lo, hi, engine):
+            if (g, x) not in y_in:
+                y_in[g, x] = work.tile([P, PACK * D], BF16, name="y_in", bufs=Y_IN_BUFS, align_bytes=64)
+            dst = y_in[g, x][:, lo * PACK:hi * PACK]
+            src = y[g, x][:, :, lo:hi]
+            if engine == "gpsimd":
+                nc.gpsimd.tensor_scalar(
+                    out=dst.rearrange("p (d t) -> p d t", t=PACK), in0=src.rearrange("p t d -> p d t"),
+                    scalar1=1.0, scalar2=-0.0, op0=ALU.mult, op1=ALU.add,
                 )
-            elif c == CHUNKS - 1:
-                nc.sync.dma_start(out=words, in_=codes)
-            if c == CHUNKS - 1:
-                queue = nc.scalar if n == STEPS - 1 else nc.sync
-                for quad in range(4):
-                    queue.dma_start(
-                        out=out_2[g, 4 * quad:4 * quad + 4, :].bitcast(I32),
-                        in_=y_scales[g][32 * quad:32 * quad + 4, :].bitcast(I32),
-                    )
-
-        load_gscale(0, 1)
-        load_grad(0, 0, 1)
-        load_w(0)
-        load_w(1)
-        load_grad(0, 1, PASSES)
-        for item in LOADS.split():
-            i = int(item[1])
-            if item[0] == "w":
-                load_w(i)
-            elif item[0] == "s":
-                load_gscale(1, GROUPS)
-            elif item[0] == "g":
-                load_grad(i, 0, PASSES)
-            elif item[0] == "a":
-                load_tokens(a, a_sb, "a_sb", i, 4)
             else:
-                load_tokens(b, b_sb, "b_sb", i, 3)
+                copy = nc.vector.tensor_copy if engine == "vector" else nc.scalar.copy
+                copy(
+                    out=dst.rearrange("p (m i t) -> p m t i", i=RUN, t=PACK),
+                    in_=src.rearrange("p t (m i) -> p m t i", i=RUN),
+                )
 
-        last_piece = len(W_PIECES) - 1
-        ahead = len(SIG_TICKS)
+        def quantize_y(g, x, lo, hi):
+            if g not in y_codes:
+                y_codes[g] = work.tile([P, 2 * D], U32, name="y_codes", align_bytes=64)
+                y_scales[g] = work.tile([P, 2 * D], U8, name="y_scales", align_bytes=64)
+            cols = slice(x * D + lo, x * D + hi)
+            nc.vector.quantize_mx(
+                out=y_codes[g][:, cols].bitcast(E4M3X4), scales=y_scales[g][:, cols],
+                in_=y_in[g, x][:, lo * PACK:hi * PACK],
+            )
+
+        def quantize_half(g, x):
+            quantize_y(g, x, 0, 2 * W)
+            quantize_y(g, x, 2 * W, D)
+
+        def store_codes(g, lo, hi):
+            words = out_1[g].rearrange("p m t -> p (m t)").bitcast(I32)
+            nc.sync.dma_start(out=words[:, lo:hi], in_=y_codes[g][:, lo:hi].bitcast(I32))
+
+        def store_scales(g):
+            for quad in range(QUADS):
+                queue = nc.scalar if g == LAST and quad > 0 else nc.sync
+                queue.dma_start(
+                    out=out_2[g, 4 * quad:4 * quad + 4, :].bitcast(I32),
+                    in_=y_scales[g][32 * quad:32 * quad + 4, :].bitcast(I32),
+                )
+
+        def finish_planes(g):
+            quantize_half(g, 0)
+            quantize_half(g, 1)
+            store_codes(g, 0, 2 * D)
+            store_scales(g)
+
+        load_b(0, 0, W)
+        sigmoid(0, 0, 0, 1)
+        load_gscale(0, 2)
+        load_grad(0, 0, 1)
+        load_w(0, 0, W)
+        load_w(0, W, D)
+        load_grad(0, 1, 2)
+        load_w(0, D, TAPS * D)
+        load_grad(0, 2, 3)
+        load_w(1, 0, D)
+        load_grad(1, 0, PASSES)
+        load_w(1, D, TAPS * D)
+        load_b(0, W)
+        load_w(2, 0, D)
+        load_w(2, D, TAPS * D)
+        load_gscale(2, GROUPS)
+        load_grad(2, 0, PASSES)
+        load_a(0)
+        load_b(1)
+        load_grad(3, 0, PASSES)
+        load_a(1)
+        load_b(2)
+        load_a(2)
+        load_a(3)
+
+        last_piece = len(w_raw) - 1
         interleave_w(0)
+        quantize_w(0)
         for u in range(HEAD_UNITS):
             scale_grad(u)
             if u > 0:
                 copy_grad(u - 1)
-            if u in SIG_TICKS:
-                sigmoid(SIG_TICKS.index(u))
-            if u == 0:
-                quantize_w(0)
+            if u in SIGMOID_TICKS:
+                c = SIGMOID_TICKS.index(u)
+                sigmoid(0, c, 1 if c == 0 else 0)
             if u < last_piece:
                 interleave_w(u + 1)
-                if u > 0:
-                    quantize_w(u)
+            if u == 0:
+                quantize_w(1)
+            if 1 < u < last_piece:
+                quantize_w(u)
             if u == last_piece:
-                quantize_w(last_piece, 0, 1)
-                gate_factor(0)
-                quantize_w(last_piece, 1, CHUNKS)
+                quantize_w(u, 0, 1)
+                gate_factor(0, 0)
+                quantize_w(u, 1)
             if u > 1:
                 quantize_grad(u - 2)
             if u == HEAD_UNITS - 1:
-                multiply(0)
+                multiply(0, PASSES - 1)
             turn_grad(u)
+            if u in EARLY_PASS_TICKS:
+                s = EARLY_PASS_TICKS.index(u)
+                multiply(0, s, s + 1)
+        copy_grad(HEAD_UNITS - 1)
+        load_b(LAST)
 
-        for n in range(STEPS):
-            last = n == STEPS - 1
-            if not last:
-                multiply(n + 1)
-            if n > 0:
-                interleave_y(n - 1, 1, False)
-            if n == 0 or (n - 1) % UNIT_STRIDE == 0:
-                fresh = HEAD_UNITS - 1 if n == 0 else HEAD_UNITS + (n - 1) // UNIT_STRIDE
-                if fresh < UNITS:
-                    copy_grad(fresh)
-            if n % UNIT_STRIDE == 0 and HEAD_UNITS + n // UNIT_STRIDE < UNITS:
-                scale_grad(HEAD_UNITS + n // UNIT_STRIDE)
-                turn_grad(HEAD_UNITS + n // UNIT_STRIDE)
-            if n + ahead < STEPS:
-                sigmoid(n + ahead)
-            if n == 0:
-                load_tokens(b, b_sb, "b_sb", 3, 3)
-            value_half(n)
-            if not last:
-                gate_factor(n + 1)
-            else:
-                quantize_y(n - 1, 0)
-            if n not in VECTOR_STEPS:
-                interleave_y(n, 0, False)
-            gate_half(n)
-            if n in VECTOR_STEPS:
-                interleave_y(n, 0, True)
-            if n > 0:
-                if not last:
-                    quantize_y(n - 1, 0)
-                quantize_y(n - 1, 1)
-                store_planes(n - 1)
-            if n == 0:
-                quantize_grad(HEAD_UNITS - 2)
-                quantize_grad(HEAD_UNITS - 1)
-            elif (n - 1) % UNIT_STRIDE == 0 and HEAD_UNITS + (n - 1) // UNIT_STRIDE < UNITS:
-                quantize_grad(HEAD_UNITS + (n - 1) // UNIT_STRIDE)
-        interleave_y(STEPS - 1, 1, True)
-        quantize_y(STEPS - 1, 0)
-        quantize_y(STEPS - 1, 1)
-        store_planes(STEPS - 1)
+        def open_round(g):
+            if g > 0:
+                interleave_y(g - 1, 1, D - GPSIMD_COLS, D, "gpsimd")
+                interleave_y(g - 1, 1, 0, D - GPSIMD_COLS, "scalar")
+            value_half(g)
+
+        quantised = HEAD_UNITS - 2
+        for g in range(LAST):
+            copied = min(HEAD_UNITS + UNITS_PER_ROUND * g, UNITS)
+            units = range(copied, min(copied + UNITS_PER_ROUND, UNITS))
+            open_round(g)
+            for u in range(quantised, (g + 2) * PASSES):
+                quantize_grad(u)
+            quantised = (g + 2) * PASSES
+            if g > 0:
+                gate_factor(g, 0)
+            gate_factor(g, 1)
+            multiply(g + 1)
+            for c in range(CHUNKS):
+                if c < len(units):
+                    scale_grad(units[c])
+                    turn_grad(units[c])
+                sigmoid(g + 1, c)
+                if 0 < c <= len(units):
+                    copy_grad(units[c - 1])
+            interleave_y(g, 0, 0, D, "scalar")
+            gate_half(g, 0, W)
+            gate_half(g, W, 2 * W)
+            store_y(g, 1, 0, 2 * W)
+            gate_factor(g, 2)
+            if g > 0:
+                finish_planes(g - 1)
+            for u in range(quantised, copied):
+                quantize_grad(u)
+            quantised = max(quantised, copied)
+            gate_half(g, 2 * W, D)
+            store_y(g, 1, 2 * W, D)
+
+        mid = D - W // 2
+        open_round(LAST)
+        for c in range(CHUNKS):
+            interleave_y(LAST, 0, c * W, (c + 1) * W, "scalar")
+        gate_factor(LAST, 0)
+        gate_factor(LAST, 1)
+        finish_planes(LAST - 1)
+        for c in range(2):
+            gate_half(LAST, c * W, (c + 1) * W)
+            store_y(LAST, 1, c * W, (c + 1) * W)
+            interleave_y(LAST, 1, c * W, (c + 1) * W, "scalar")
+        gate_factor(LAST, 2)
+        quantize_half(LAST, 0)
+        store_codes(LAST, 0, D)
+        gate_half(LAST, 2 * W, mid)
+        interleave_y(LAST, 1, 2 * W, mid, "scalar")
+        gate_half(LAST, mid, D)
+        store_y(LAST, 1, 2 * W, D)
+        quantize_y(LAST, 1, 0, 2 * W)
+        store_codes(LAST, D, D + 2 * W)
+        interleave_y(LAST, 1, mid, D, "vector")
+        quantize_y(LAST, 1, 2 * W, mid)
+        quantize_y(LAST, 1, mid, D)
+        store_codes(LAST, D + 2 * W, 2 * D)
+        store_scales(LAST)

from contextlib import ExitStack

import concourse.mybir as mybir
from concourse.masks import make_identity

R, K, D, TAPS = 1024, 1536, 768, 2
FLOPS = 2 * R * K * TAPS * D

F32 = mybir.dt.float32
BF16 = mybir.dt.bfloat16
I32 = mybir.dt.int32
U32 = mybir.dt.uint32
U8 = mybir.dt.uint8
FP8 = mybir.dt.float8_e4m3fn
E4M3X4 = mybir.dt.float8_e4m3fn_x4
E5M2X4 = mybir.dt.float8_e5m2_x4
ACT = mybir.ActivationFunctionType
ALU = mybir.AluOpType

P = 128
PACK = 4
KP = P * PACK
PASSES = K // KP
BLOCK = 32
GROUPS = R * TAPS // KP
LAST = GROUPS - 1
ROWS = PACK // TAPS
PAIRS = PACK // 2
W = 256
CHUNKS = D // W
UNITS = GROUPS * PASSES
QUADS = 4
RUN = 4

HEAD_UNITS = 8
SIGMOID_TICKS = (4, 6, 7)
EARLY_PASS_TICKS = (4, 5)
UNITS_PER_ROUND = 2
GPSIMD_COLS = D // 2

WIDE_BUFS = 4
ACC_BUFS = ROWS * CHUNKS
BYTES_BUFS = 3
B_BUFS = 3
H_BUFS = CHUNKS + 1
G_ROWS_BUFS = 3
G_IN_BUFS = 4
Y_IN_BUFS = 3


def tile_strided_conv_glu_backward_b13_kernel(tc, grad_bytes, grad_scale, w, a, b, out_0, out_1, out_2):
    nc = tc.nc
    with ExitStack() as ctx:
        keep = ctx.enter_context(tc.tile_pool(name="keep", bufs=1))
        work = ctx.enter_context(tc.tile_pool(name="work", bufs=2))
        psum = ctx.enter_context(tc.psum_pool(name="psum", bufs=2))
        ctx.enter_context(tc.manual_schedule())

        ident = keep.tile([P, P], F32, name="ident")
        make_identity(nc, ident[:])

        w_codes = keep.tile([P, PASSES * TAPS * D], U32, name="w_codes", align_bytes=64)
        w_scales = keep.tile([P, PASSES * TAPS * D], U8, name="w_scales", align_bytes=64)
        g_codes = keep.tile([P, UNITS * ROWS * P], U32, name="g_codes", align_bytes=64)
        g_scales = keep.tile([P, UNITS * ROWS * P], U8, name="g_scales", align_bytes=64)

        gbytes, gscale, a_sb, b_sb = {}, {}, {}, {}
        w_raw, w_in, g_rows, g_bank, g_in = [], {}, {}, {}, {}
        acc, h, q, y, y_in, y_codes, y_scales = {}, {}, {}, {}, {}, {}, {}

        def load_grad(g, s0, s1):
            piece = work.tile([P, ROWS, (s1 - s0) * KP], U8, name="gbytes" if g else "gbytes_head", bufs=BYTES_BUFS)
            rows = grad_bytes[g * ROWS * P:(g + 1) * ROWS * P, s0 * KP:s1 * KP]
            nc.sync.dma_start(out=piece[:], in_=rows.rearrange("(p e) k -> p e k", e=ROWS))
            for s in range(s0, s1):
                gbytes[g * PASSES + s] = piece[:, :, (s - s0) * KP:(s - s0 + 1) * KP]

        def load_gscale(g0, g1):
            piece = keep.tile([P, g1 - g0, ROWS * K // BLOCK], F32, name="gscale%d" % g0)
            rows = grad_scale[g0 * ROWS * P:g1 * ROWS * P, :]
            nc.sync.dma_start(out=piece[:], in_=rows.rearrange("(g p e) c -> p g (e c)", p=P, e=ROWS))
            for g in range(g0, g1):
                gscale[g] = piece[:, g - g0, :]

        def load_w(s, lo, hi):
            if s == 0:
                piece = keep.tile([P, PACK, hi - lo], BF16, name="w_first%d" % lo)
            else:
                piece = work.tile([P, PACK, hi - lo], BF16, name="w_pass", tag="wide", bufs=WIDE_BUFS)
            rows = w[s * KP:(s + 1) * KP, lo:hi]
            nc.sync.dma_start(out=piece[:], in_=rows.rearrange("(p t) n -> p t n", t=PACK))
            w_raw.append((s, lo, hi, piece))

        def load_tokens(src, tiles, name, bufs, g, lo=0, hi=PACK * D):
            if lo == 0:
                tiles[g] = work.tile([P, PACK, D], BF16, name=name, bufs=bufs)
            rows = src[g * KP:(g + 1) * KP, :].rearrange("(p t) d -> p (t d)", t=PACK)
            nc.sync.dma_start(out=tiles[g][:].rearrange("p t d -> p (t d)")[:, lo:hi], in_=rows[:, lo:hi])

        def load_a(g):
            load_tokens(a, a_sb, "a_sb", GROUPS, g)

        def load_b(g, lo=0, hi=PACK * D):
            load_tokens(b, b_sb, "b_sb", B_BUFS, g, lo, hi)

        def interleave_w(i):
            s, lo, hi, piece = w_raw[i]
            w_in[i] = work.tile([P, PACK * (hi - lo)], BF16, name="w_in", align_bytes=64)
            nc.vector.tensor_copy(
                out=w_in[i][:].rearrange("p (m i t) -> p m t i", i=RUN, t=PACK),
                in_=piece[:].rearrange("p t (m i) -> p m t i", i=RUN),
            )

        def quantize_w(i, first=0, stop=CHUNKS):
            s, lo, hi, piece = w_raw[i]
            for m in range(first, min(stop, (hi - lo) // W)):
                j, c = divmod(lo // W + m, CHUNKS)
                at = ((s * CHUNKS + c) * TAPS + j) * W
                nc.vector.quantize_mx(
                    out=w_codes[:, at:at + W].bitcast(E4M3X4),
                    scales=w_scales[:, at:at + W],
                    in_=w_in[i][:, m * W * PACK:(m + 1) * W * PACK],
                )

        def scale_grad(u):
            g, s = divmod(u, PASSES)
            g_rows[u] = work.tile([P, ROWS * KP], BF16, name="g_rows", bufs=G_ROWS_BUFS)
            for e in range(ROWS):
                for m in range(KP // BLOCK):
                    col = (e * K + s * KP) // BLOCK + m
                    nc.scalar.activation(
                        out=g_rows[u][:, e * KP + m * BLOCK:e * KP + (m + 1) * BLOCK],
                        in_=gbytes[u][:, e, m * BLOCK:(m + 1) * BLOCK].bitcast(FP8),
                        func=ACT.Copy,
                        scale=gscale[g][:, col:col + 1],
                    )

        def turn_grad(u):
            g_bank[u] = psum.tile([P, ROWS * PAIRS, P], F32, name="g_bank")
            words = g_rows[u][:].bitcast(F32)
            for e in range(ROWS):
                for v in range(PAIRS):
                    nc.tensor.transpose(
                        g_bank[u][:, PAIRS * e + v, :], words[:, e * PAIRS * P + v:(e + 1) * PAIRS * P:PAIRS], ident[:]
                    )

        def copy_grad(u):
            g_in[u] = work.tile([P, ROWS * KP], BF16, name="g_in", bufs=G_IN_BUFS, align_bytes=64)
            nc.scalar.copy(
                out=g_in[u][:].bitcast(F32).rearrange("p (e r v) -> p e r v", e=ROWS, v=PAIRS),
                in_=g_bank[u][:].rearrange("p (e v) r -> p e r v", v=PAIRS),
            )

        def quantize_grad(u):
            cols = slice(u * ROWS * P, (u + 1) * ROWS * P)
            nc.vector.quantize_mx(out=g_codes[:, cols].bitcast(E5M2X4), scales=g_scales[:, cols], in_=g_in[u][:])

        def banks(g):
            if g == LAST:
                return [(e, c) for e in range(ROWS) for c in range(CHUNKS)]
            return [(e, c) for c in range(CHUNKS) for e in range(ROWS)]

        def multiply(g, s0=0, s1=PASSES):
            for e, c in banks(g):
                if s0 == 0:
                    acc[g, e, c] = psum.tile([P, TAPS * W], F32, name="acc", bufs=ACC_BUFS)
                for s in range(s0, s1):
                    rows = ((g * PASSES + s) * ROWS + e) * P
                    at = (s * CHUNKS + c) * TAPS * W
                    nc.tensor.matmul_mx(
                        out=acc[g, e, c][:],
                        lhsT=g_codes[:, rows:rows + P].bitcast(E5M2X4),
                        lhsT_scale=g_scales[:, rows:rows + P],
                        rhs=w_codes[:, at:at + TAPS * W].bitcast(E4M3X4),
                        rhs_scale=w_scales[:, at:at + TAPS * W],
                        start=(s == 0),
                        stop=(s == PASSES - 1),
                    )

        def sigmoid(g, c, t0=0, t1=PACK):
            if t0 == 0:
                h[g, c] = work.tile([P, PACK, W], F32, name="h", bufs=H_BUFS)
            nc.scalar.activation(out=h[g, c][:, t0:t1, :], in_=b_sb[g][:, t0:t1, c * W:(c + 1) * W], func=ACT.Sigmoid)

        def gate_factor(g, c):
            q[g, c] = work.tile([P, PACK, W], F32, name="q")
            nc.vector.scalar_tensor_tensor(
                out=q[g, c][:], in0=h[g, c][:], scalar=1.0, in1=a_sb[g][:, :, c * W:(c + 1) * W],
                op0=ALU.subtract, op1=ALU.mult,
            )

        def store_y(g, x, lo, hi, t0=0, t1=PACK):
            rows = out_0[g * KP:(g + 1) * KP, x * D + lo:x * D + hi].rearrange("(p t) d -> p t d", t=PACK)
            nc.sync.dma_start(out=rows[:, t0:t1, :], in_=y[g, x][:, t0:t1, lo:hi])

        def value_half(g):
            y[g, 0] = work.tile([P, PACK, D], F32, name="da", tag="wide", bufs=WIDE_BUFS)
            for e, c in banks(g):
                nc.vector.tensor_tensor(
                    out=y[g, 0][:, e * TAPS:(e + 1) * TAPS, c * W:(c + 1) * W],
                    in0=acc[g, e, c][:].rearrange("p (j d) -> p j d", j=TAPS),
                    in1=h[g, c][:, e * TAPS:(e + 1) * TAPS, :],
                    op=ALU.mult,
                )
                if c == CHUNKS - 1:
                    store_y(g, 0, 0, D, e * TAPS, (e + 1) * TAPS)

        def gate_half(g, lo, hi):
            c = lo // W
            if lo == 0:
                y[g, 1] = work.tile([P, PACK, D], F32, name="db", tag="wide", bufs=WIDE_BUFS)
            nc.vector.scalar_tensor_tensor(
                out=y[g, 1][:, :, lo:hi], in0=y[g, 0][:, :, lo:hi], scalar=-1.0,
                in1=q[g, c][:, :, lo - c * W:hi - c * W], op0=ALU.mult, op1=ALU.mult,
            )

        def interleave_y(g, x, lo, hi, engine):
            if (g, x) not in y_in:
                y_in[g, x] = work.tile([P, PACK * D], BF16, name="y_in", bufs=Y_IN_BUFS, align_bytes=64)
            dst = y_in[g, x][:, lo * PACK:hi * PACK]
            src = y[g, x][:, :, lo:hi]
            if engine == "gpsimd":
                nc.gpsimd.tensor_scalar(
                    out=dst.rearrange("p (d t) -> p d t", t=PACK), in0=src.rearrange("p t d -> p d t"),
                    scalar1=1.0, scalar2=-0.0, op0=ALU.mult, op1=ALU.add,
                )
            else:
                copy = nc.vector.tensor_copy if engine == "vector" else nc.scalar.copy
                copy(
                    out=dst.rearrange("p (m i t) -> p m t i", i=RUN, t=PACK),
                    in_=src.rearrange("p t (m i) -> p m t i", i=RUN),
                )

        def quantize_y(g, x, lo, hi):
            if g not in y_codes:
                y_codes[g] = work.tile([P, 2 * D], U32, name="y_codes", align_bytes=64)
                y_scales[g] = work.tile([P, 2 * D], U8, name="y_scales", align_bytes=64)
            cols = slice(x * D + lo, x * D + hi)
            nc.vector.quantize_mx(
                out=y_codes[g][:, cols].bitcast(E4M3X4), scales=y_scales[g][:, cols],
                in_=y_in[g, x][:, lo * PACK:hi * PACK],
            )

        def quantize_half(g, x):
            quantize_y(g, x, 0, 2 * W)
            quantize_y(g, x, 2 * W, D)

        def store_codes(g, lo, hi):
            words = out_1[g].rearrange("p m t -> p (m t)").bitcast(I32)
            nc.sync.dma_start(out=words[:, lo:hi], in_=y_codes[g][:, lo:hi].bitcast(I32))

        def store_scales(g):
            for quad in range(QUADS):
                queue = nc.scalar if g == LAST and quad > 0 else nc.sync
                queue.dma_start(
                    out=out_2[g, 4 * quad:4 * quad + 4, :].bitcast(I32),
                    in_=y_scales[g][32 * quad:32 * quad + 4, :].bitcast(I32),
                )

        def finish_planes(g):
            quantize_half(g, 0)
            quantize_half(g, 1)
            store_codes(g, 0, 2 * D)
            store_scales(g)

        load_b(0, 0, W)
        sigmoid(0, 0, 0, 1)
        load_gscale(0, 2)
        load_grad(0, 0, 1)
        load_w(0, 0, W)
        load_w(0, W, D)
        load_grad(0, 1, 2)
        load_w(0, D, TAPS * D)
        load_grad(0, 2, 3)
        load_w(1, 0, D)
        load_grad(1, 0, PASSES)
        load_w(1, D, TAPS * D)
        load_b(0, W)
        load_w(2, 0, D)
        load_w(2, D, TAPS * D)
        load_gscale(2, GROUPS)
        load_grad(2, 0, PASSES)
        load_a(0)
        load_b(1)
        load_grad(3, 0, PASSES)
        load_a(1)
        load_b(2)
        load_a(2)
        load_a(3)

        last_piece = len(w_raw) - 1
        interleave_w(0)
        quantize_w(0)
        for u in range(HEAD_UNITS):
            scale_grad(u)
            if u > 0:
                copy_grad(u - 1)
            if u in SIGMOID_TICKS:
                c = SIGMOID_TICKS.index(u)
                sigmoid(0, c, 1 if c == 0 else 0)
            if u < last_piece:
                interleave_w(u + 1)
            if u == 0:
                quantize_w(1)
            if 1 < u < last_piece:
                quantize_w(u)
            if u == last_piece:
                quantize_w(u, 0, 1)
                gate_factor(0, 0)
                quantize_w(u, 1)
            if u > 1:
                quantize_grad(u - 2)
            if u == HEAD_UNITS - 1:
                multiply(0, PASSES - 1)
            turn_grad(u)
            if u in EARLY_PASS_TICKS:
                s = EARLY_PASS_TICKS.index(u)
                multiply(0, s, s + 1)
        copy_grad(HEAD_UNITS - 1)
        load_b(LAST)

        def open_round(g):
            if g > 0:
                interleave_y(g - 1, 1, D - GPSIMD_COLS, D, "gpsimd")
                interleave_y(g - 1, 1, 0, D - GPSIMD_COLS, "scalar")
            value_half(g)

        quantised = HEAD_UNITS - 2
        for g in range(LAST):
            copied = min(HEAD_UNITS + UNITS_PER_ROUND * g, UNITS)
            units = range(copied, min(copied + UNITS_PER_ROUND, UNITS))
            open_round(g)
            for u in range(quantised, (g + 2) * PASSES):
                quantize_grad(u)
            quantised = (g + 2) * PASSES
            if g > 0:
                gate_factor(g, 0)
            gate_factor(g, 1)
            multiply(g + 1)
            for c in range(CHUNKS):
                if c < len(units):
                    scale_grad(units[c])
                    turn_grad(units[c])
                sigmoid(g + 1, c)
                if 0 < c <= len(units):
                    copy_grad(units[c - 1])
            interleave_y(g, 0, 0, D, "scalar")
            gate_half(g, 0, W)
            gate_half(g, W, 2 * W)
            store_y(g, 1, 0, 2 * W)
            gate_factor(g, 2)
            if g > 0:
                finish_planes(g - 1)
            for u in range(quantised, copied):
                quantize_grad(u)
            quantised = max(quantised, copied)
            gate_half(g, 2 * W, D)
            store_y(g, 1, 2 * W, D)

        mid = D - W // 2
        open_round(LAST)
        for c in range(CHUNKS):
            interleave_y(LAST, 0, c * W, (c + 1) * W, "scalar")
        gate_factor(LAST, 0)
        gate_factor(LAST, 1)
        finish_planes(LAST - 1)
        for c in range(2):
            gate_half(LAST, c * W, (c + 1) * W)
            store_y(LAST, 1, c * W, (c + 1) * W)
            interleave_y(LAST, 1, c * W, (c + 1) * W, "scalar")
        gate_factor(LAST, 2)
        quantize_half(LAST, 0)
        store_codes(LAST, 0, D)
        gate_half(LAST, 2 * W, mid)
        interleave_y(LAST, 1, 2 * W, mid, "scalar")
        gate_half(LAST, mid, D)
        store_y(LAST, 1, 2 * W, D)
        quantize_y(LAST, 1, 0, 2 * W)
        store_codes(LAST, D, D + 2 * W)
        interleave_y(LAST, 1, mid, D, "vector")
        quantize_y(LAST, 1, 2 * W, mid)
        quantize_y(LAST, 1, mid, D)
        store_codes(LAST, D + 2 * W, 2 * D)
        store_scales(LAST)
